import numpy as np, ml_dtypes
CORES = [24,25,26,27,28,29,30,31,224,225,226,227,228,229,230,231]
N = 16
KB, QP = 1, 256
ROOT = 9
def setup_inputs(rng):
    q = rng.standard_normal((N, 128, QP), dtype=np.float32) / 4; k = rng.standard_normal((N, 128, KB * 128), dtype=np.float32)
    a = 2 * np.pi * rng.random((N, QP)); s = 400 * rng.random((N, QP)) ** 1.5; q[:, 0, :] = s * np.cos(a); q[:, 1, :] = s * np.sin(a); q[:, 2, :] = 150 * rng.standard_normal((N, QP)); k[:, 2, :] = 1 + k[:, 2, :] / 50
    a = (2 * np.pi * rng.random() + np.pi / 2 * (rng.permutation(N).reshape(N, 1, 1) + 0.5) / N - 0.5 + (np.arange(KB).reshape(1, KB, 1) + rng.random((N, KB, 128))) / KB).reshape(N, KB * 128); k[:, 0, :] = np.cos(a); k[:, 1, :] = np.sin(a)
    for t in range(0, QP, 2):
        j, i = (t // 2) % N, rng.integers(KB * 128); q[ROOT, :2, t] = s[ROOT, t] * k[j, :2, i]; q[ROOT, 3:, t] += k[j, 3:, i] / 8
    return {"q": q.astype(ml_dtypes.bfloat16), "k": k.astype(ml_dtypes.bfloat16), "v": rng.standard_normal((N, 128, KB * 128), dtype=np.float32).astype(ml_dtypes.bfloat16)}
def setup_inputs_big(rng):
    d = setup_inputs(rng)
    for k in ("v",): d[k] = (d[k].astype(np.float32) * 1048576.0).astype(d[k].dtype)
    return d
def setup_inputs_small(rng):
    d = setup_inputs(rng)
    for k in ("v",): d[k] = (d[k].astype(np.float32) * (1 / 1048576.0)).astype(d[k].dtype)
    return d
def reference(q, k, v):
    Q, K, V = q.astype(np.float64), k.astype(np.float64), v.astype(np.float64)
    y = np.full((N, QP, 128), np.nan)
    for r in [ROOT]:
        js = list(range(N))
        S = np.concatenate([K[j].T @ Q[r] for j in js], axis=0)
        P = np.exp(S - S.max(axis=0)); P = P / P.sum(axis=0)
        y[r] = P.T @ np.concatenate([V[j][:, 128 * b:128 * b + 128] for j in js for b in range(KB)], axis=0)
    return {"y": y.astype(ml_dtypes.bfloat16)}

@@ -1,0 +1,271 @@
+from concourse.bass import DstId, RemoteDMATransfer
+from concourse.mybir import AluOpType, AxisListType, ActivationFunctionType
+
+BW = 264
+SW = 264
+NSLOT = 6
+
+SCRATCH = {
+    "qs": ("sbuf", [128, 256], "bfloat16"),
+    "kvd": ("dram", [128, 256], "bfloat16"),
+    "rly": ("dram", [128, 256], "bfloat16"),
+    "kvA": ("sbuf", [128, 4 * BW], "bfloat16"),
+    "kvL": ("sbuf", [128, 4 * BW], "bfloat16"),
+    "onesb": ("sbuf", [128, 128], "bfloat16"),
+    "ident": ("sbuf", [128, 128], "bfloat16"),
+    "pT": ("sbuf", [128, 4 * 512], "bfloat16"),
+    "pK": ("sbuf", [128, 4 * 512], "bfloat16"),
+    "part": ("sbuf", [128, NSLOT * SW], "bfloat16"),
+    "msg": ("sbuf", [128, SW], "bfloat16"),
+    "nmo": ("sbuf", [128, 16], "bfloat16"),
+    "wo": ("sbuf", [128, 8], "float32"),
+    "dgo": ("sbuf", [128, 256], "bfloat16"),
+    "gM": ("sbuf", [128, 8], "float32"),
+    "wj": ("sbuf", [128, 16], "float32"),
+    "rc": ("sbuf", [128, 8], "float32"),
+    "dg": ("sbuf", [128, 2 * NSLOT * 128], "bfloat16"),
+    "ys": ("sbuf", [128, 256], "bfloat16"),
+    "sS0": ("psum", [128, 512], "float32"),
+    "sS1": ("psum", [128, 512], "float32"),
+    "tP0": ("psum", [128, 1024], "bfloat16"),
+    "tP1": ("psum", [128, 1024], "bfloat16"),
+    "oP0": ("psum", [128, 512], "float32"),
+    "oP1": ("psum", [128, 512], "float32"),
+    "tF0": ("psum", [128, 512], "float32"),
+    "tF1": ("psum", [128, 512], "float32"),
+}
+SEMAPHORES = (["ld", "ldq", "arrQ", "arrA", "arrL", "arrR", "arrP", "sent", "ms", "idn", "st"]
+              + ["%s%s%d" % (s, p, b) for s in "SREFTCOP" for p in "AL" for b in (0, 1)]
+              + ["%sA%d" % (s, b) for s in "UVXWDGH" for b in (0, 1)]
+              + ["%s%d" % (s, b) for s in ("gm", "gw", "gd", "ga", "gr", "gy") for b in (0, 1)])
+
+
+def _bits(mask):
+    return bin(mask).count("1")
+
+
+def _roles(T, topo):
+    root = T.cores[T.root]
+    near = [c for c in T.cores if topo.host(c) == topo.host(root) and topo.chip(c) == topo.chip(root)]
+    far = [c for c in T.cores if c not in near]
+    ports = [c for c in far if topo.may_write(c, root)]
+    plain = [c for c in far if c not in ports]
+    relay, helper = {}, {}
+    for d in sorted(set(topo.die(c) for c in far)):
+        pd = [c for c in ports if topo.die(c) == d]
+        for a, p in zip([c for c in plain if topo.die(c) == d], pd):
+            relay[a] = p
+        cand = [c for c in near if c != root and topo.die(c) == d]
+        for p, h in zip(pd, cand[len(cand) - len(pd):]):
+            helper[p] = h
+    helpers = [helper[p] for p in ports]
+    locals_ = [c for c in near if c != root and c not in helpers]
+    return root, ports, plain, relay, helper, helpers, locals_
+
+
+def rank_program(g, core, T, topo):
+    if T.rank_of(core) is None:
+        return
+    root, ports, plain, relay, helper, helpers, locals_ = _roles(T, topo)
+    tot = {}
+
+    def inc(ins, name, n=1):
+        ins.then_inc(T.sem[name], n)
+        tot[name] = tot.get(name, 0) + n
+
+    def wait(q, *names):
+        for name in names:
+            if name in tot:
+                q.wait_ge(T.sem[name], tot[name])
+
+    def send(dst, out_ap, in_ap, rsem):
+        rid, pid = topo.addr(dst, core)
+        m = topo.mask(core, dst)
+        g.remote_dma(out_ap=out_ap, in_ap=in_ap, remote_sem=T.sem[rsem], local_sem=T.sem.sent, pid=pid,
+                     routing_id=rid, dma_engine_mask=m)
+        tot["sent"] = tot.get("sent", 0) + _bits(m)
+
+    if core in plain or core in ports:
+        inc(g.sync.dma_start(T.kvd[:, 0:128], T.k[:, :]), "ld", 16)
+        inc(g.scalar.dma_start(T.kvd[:, 128:256], T.v[:, :]), "ld", 16)
+        wait(g, "ld")
+        if core in plain:
+            send(relay[core], T.rly[:, :], T.kvd[:, :], "arrR")
+        else:
+            send(helper[core], T.kvA[:, BW:BW + 256], T.kvd[:, :], "arrA")
+            src = [a for a in plain if relay[a] == core][0]
+            tot["arrR"] = _bits(topo.mask(src, core))
+            wait(g, "arrR")
+            s = plain.index(src)
+            send(root, T.kvL[:, s * BW:s * BW + 256], T.rly[:, :], "arrL")
+        wait(g, "sent")
+        return
+
+    if core in locals_:
+        inc(g.sync.dma_start(T.kvA[:, 0:128], T.k[:, :]), "ld", 16)
+        inc(g.scalar.dma_start(T.kvA[:, 128:256], T.v[:, :]), "ld", 16)
+        wait(g, "ld")
+        s = 1 + locals_.index(core)
+        send(root, T.kvA[:, s * BW:s * BW + 256], T.kvA[:, 0:256], "arrA")
+        wait(g, "sent")
+        return
+
+    is_root = core == root
+    pe, dve, act = g.tensor, g.vector, g.scalar
+    sS, tP, oP, tF = [T.sS0, T.sS1], [T.tP0, T.tP1], [T.oP0, T.oP1], [T.tF0, T.tF1]
+    Exp = ActivationFunctionType.Exp
+    nA = 1 + len(locals_) if is_root else 2
+
+    if is_root:
+        inc(g.sync.dma_start(T.qs[:, :], T.q[:, :]), "ldq", 16)
+    inc(g.scalar.dma_start(T.kvA[:, 0:128], T.k[:, :]), "ld", 16)
+    inc(g.sync.dma_start(T.kvA[:, 128:256], T.v[:, :]), "ld", 16)
+
+    inc(dve.memset(T.onesb[:, :], 1.0), "ms")
+    for i in range(nA):
+        inc(dve.memset(T.kvA[:, i * BW + 256:(i + 1) * BW], 1.0), "ms")
+    if is_root:
+        for i in range(len(plain)):
+            inc(dve.memset(T.kvL[:, i * BW + 256:(i + 1) * BW], 1.0), "ms")
+    else:
+        inc(dve.memset(T.msg[:, 260:SW], 0.0), "ms")
+    wait(g, "ms")
+    inc(g.affine_select(T.ident[:, :], T.onesb[:, :], [[-1, 128]], AluOpType.is_equal, 0.0, 0, 1), "idn")
+
+    if is_root:
+        wait(g, "ldq")
+        m = topo.mask(core, helpers[0])
+        ids = [topo.addr(h, core) for h in helpers]
+        g.remote_dma_fused([RemoteDMATransfer(dst_ids=[DstId(rid=r, pnc=p) for r, p in ids], dma_engine_mask=m,
+                                              remote_sem=T.sem.arrQ, srcs=[T.qs[:, :]],
+                                              dsts=[T.qs[:, :] for h in helpers], alu_op=0)], local_sem=T.sem.sent)
+        tot["sent"] = _bits(m)
+        qsem = "ldq"
+        tot["arrA"] = sum(_bits(topo.mask(c, core)) for c in locals_)
+        tot["arrL"] = sum(_bits(topo.mask(relay[a], core)) for a in plain)
+        tot["arrP"] = sum(_bits(topo.mask(h, core)) for h in helpers)
+    else:
+        qsem = "arrQ"
+        tot["arrQ"] = _bits(topo.mask(root, core))
+        tot["arrA"] = _bits(topo.mask([p for p in ports if helper[p] == core][0], core))
+
+    def group(ph, pi, kv, nb, dst, off, data, before, own):
+        n = nb * 128
+        f = 1 if own else 0
+        mid = f + (nb - f) // 2
+        pieces = [(a, z, s) for a, z, s in ((f, mid, "E"), (mid, nb, "F")) if z > a]
+        pT = [T.pT[:, (2 * pi + b) * 512:(2 * pi + b) * 512 + n] for b in (0, 1)]
+        pK = [T.pK[:, (2 * pi + b) * 512:(2 * pi + b) * 512 + n] for b in (0, 1)]
+        nm = [dst[:, off + 258 + b:off + 259 + b] for b in (0, 1)]
+        nmo = [T.nmo[:, 8 * b:8 * b + 1] for b in (0, 1)]
+        qb = [T.qs[:, b * 128:(b + 1) * 128] for b in (0, 1)]
+        k = lambda s, b: "%s%s%d" % (s, ph, b)
+        old = lambda ss, b: ["%s%s%d" % (s, before, b) for s in ss] if before else []
+        if own:
+            for b in (0, 1):
+                wait(pe, *own)
+                inc(pe.matmul(sS[b][:, 0:128], qb[b], kv[:, 0:128], True, True), k("U", b))
+            for b in (0, 1):
+                wait(dve, k("U", b))
+                inc(dve.tensor_reduce(nmo[b], sS[b][:, 0:128], AxisListType.X, AluOpType.max, negate=True), k("V", b))
+            for b in (0, 1):
+                wait(act, k("U", b), k("V", b))
+                inc(act.activation(pT[b][:, 0:128], sS[b][:, 0:128], Exp, bias=nmo[b], scale=1.0), k("X", b))
+        for b in (0, 1):
+            wait(pe, *data)
+            wait(pe, k("V", b), k("X", b), *old("USVXREF", b))
+            for i in range(f, nb):
+                inc(pe.matmul(sS[b][:, i * 128:(i + 1) * 128], qb[b], kv[:, i * BW:i * BW + 128], True, True),
+                    k("S", b))
+        for b in (0, 1):
+            wait(dve, k("S", b), k("U", b), k("X", b))
+            inc(dve.tensor_reduce(nm[b], sS[b][:, 0:n], AxisListType.X, AluOpType.max, negate=True), k("R", b))
+        for b in (0, 1):
+            wait(act, k("S", b), k("R", b))
+            if own:
+                inc(act.activation(T.wo[:, 4 * b:4 * b + 1], nmo[b], Exp, bias=nm[b], scale=-1.0), k("W", b))
+            for a, z, s in pieces:
+                inc(act.activation(pT[b][:, a * 128:z * 128], sS[b][:, a * 128:z * 128], Exp, bias=nm[b], scale=1.0),
+                    k(s, b))
+        if own:
+            for b in (0, 1):
+                wait(dve, k("W", b), "idn")
+                inc(dve.tensor_scalar(T.dgo[:, b * 128:(b + 1) * 128], T.ident[:, :], T.wo[:, 4 * b:4 * b + 1], None,
+                                      AluOpType.mult), k("D", b))
+        for b in (0, 1):
+            wait(pe, "idn", *old("TC", b))
+            if own:
+                wait(pe, k("D", b), k("X", b))
+                inc(pe.matmul(tF[b][:, 0:128], pT[b][:, 0:128], T.dgo[:, b * 128:(b + 1) * 128], True, True),
+                    k("G", b))
+            for a, z, s in pieces:
+                wait(pe, k(s, b))
+                for i in range(a, z):
+                    inc(pe.transpose(tP[b][:, i * 128:(i + 1) * 128], pT[b][:, i * 128:(i + 1) * 128],
+                                     T.ident[:, :]), k("T", b))
+        for b in (0, 1):
+            if own:
+                wait(dve, k("G", b))
+                inc(dve.tensor_copy(pK[b][:, 0:128], tF[b][:, 0:128]), k("H", b))
+            wait(dve, k("T", b))
+            inc(dve.tensor_copy(pK[b][:, f * 128:n], tP[b][:, f * 128:n]), k("C", b))
+        for b in (0, 1):
+            wait(pe, k("C", b), k("H", b), "ms", *old("OP", b))
+            for i in range(nb):
+                inc(pe.matmul(oP[b][:, 0:129], pK[b][:, i * 128:(i + 1) * 128], kv[:, i * BW + 128:i * BW + 257],
+                              i == 0, i == nb - 1), k("O", b))
+
+        def evacuate():
+            for b in (0, 1):
+                wait(act, k("O", b))
+                inc(act.activation(dst[:, off + b * 129:off + (b + 1) * 129], oP[b][:, 0:129],
+                                   ActivationFunctionType.Copy), k("P", b))
+        return evacuate
+
+    if not is_root:
+        group("A", 0, T.kvA, nA, T.msg, 0, ["arrA"], None, [qsem, "ld"])()
+        wait(g, "RA0", "RA1", "PA0", "PA1")
+        s = helpers.index(core)
+        send(root, T.part[:, s * SW:(s + 1) * SW], T.msg[:, :], "arrP")
+        wait(g, "sent")
+        return
+
+    nh = len(helpers)
+    group("A", 0, T.kvA, nA, T.part, nh * SW, ["arrA"], None, [qsem, "ld"])()
+    evac_late = group("L", 1, T.kvL, len(plain), T.part, (nh + 1) * SW, ["arrL"], "A", None)
+
+    stat = [T.part[:, 258 + b:258 + b + (NSLOT - 1) * SW + 1:SW] for b in (0, 1)]
+    for b in (0, 1):
+        wait(dve, "arrP", "RA%d" % b, "RL%d" % b)
+        inc(dve.tensor_reduce(T.gM[:, 4 * b:4 * b + 1], stat[b], AxisListType.X, AluOpType.min), "gm%d" % b)
+    for b in (0, 1):
+        wait(act, "arrP", "RA%d" % b, "RL%d" % b, "gm%d" % b)
+        inc(act.activation(T.wj[:, 8 * b:8 * b + NSLOT], stat[b], Exp, bias=T.gM[:, 4 * b:4 * b + 1], scale=-1.0),
+            "gw%d" % b)
+    evac_late()
+    for b in (0, 1):
+        wait(dve, "gw%d" % b, "idn")
+        for j in range(NSLOT):
+            c = (b * NSLOT + j) * 128
+            inc(dve.tensor_scalar(T.dg[:, c:c + 128], T.ident[:, :], T.wj[:, 8 * b + j:8 * b + j + 1], None,
+                                  AluOpType.mult), "gd%d" % b)
+    order = [nh] + list(range(nh)) + [nh + 1]
+    for b in (0, 1):
+        wait(pe, "gd%d" % b, "arrP", "PA%d" % b, "SL%d" % b, "RL%d" % b, "EL%d" % b, "FL%d" % b)
+        for x, j in enumerate(order):
+            if x == NSLOT - 1:
+                wait(pe, "PL%d" % b)
+            c = (b * NSLOT + j) * 128
+            inc(pe.matmul(sS[b][:, 0:129], T.dg[:, c:c + 128], T.part[:, j * SW + b * 129:j * SW + (b + 1) * 129],
+                          x == 0, x == NSLOT - 1), "ga%d" % b)
+    for b in (0, 1):
+        wait(dve, "ga%d" % b)
+        inc(dve.reciprocal(T.rc[:, 4 * b:4 * b + 1], sS[b][:, 128:129]), "gr%d" % b)
+        wait(dve, "gr%d" % b)
+        inc(dve.tensor_scalar(T.ys[:, b * 128:(b + 1) * 128], sS[b][:, 0:128], T.rc[:, 4 * b:4 * b + 1], None,
+                              AluOpType.mult), "gy%d" % b)
+    for b in (0, 1):
+        wait(g.sync, "gy%d" % b)
+        inc(g.sync.dma_start(T.y[b * 128:(b + 1) * 128, :], T.ys[:, b * 128:(b + 1) * 128]), "st", 16)
+    wait(g.sync, "st")
+    wait(g, "sent")

@@ -2,16 +2,21 @@ from concourse.bass import DstId, RemoteDMATransfer
 from concourse.mybir import AluOpType, AxisListType, ActivationFunctionType
 
 BW = 264
-SW = 264
+HB = 136
+SW = 2 * HB
 NSLOT = 6
 
 SCRATCH = {
     "qs": ("sbuf", [128, 256], "bfloat16"),
     "kvd": ("dram", [128, 256], "bfloat16"),
-    "rly": ("dram", [128, 256], "bfloat16"),
+    "kd": ("dram", [128, 128], "bfloat16"),
+    "vd": ("dram", [128, 128], "bfloat16"),
+    "rk": ("dram", [128, 128], "bfloat16"),
+    "rv": ("dram", [128, 128], "bfloat16"),
     "kvA": ("sbuf", [128, 4 * BW], "bfloat16"),
     "kvL": ("sbuf", [128, 4 * BW], "bfloat16"),
-    "onesb": ("sbuf", [128, 128], "bfloat16"),
+    "zero": ("sbuf", [128, 128], "bfloat16"),
+    "msk": ("sbuf", [128, 128], "bfloat16"),
     "ident": ("sbuf", [128, 128], "bfloat16"),
     "pT": ("sbuf", [128, 4 * 512], "bfloat16"),
     "pK": ("sbuf", [128, 4 * 512], "bfloat16"),
@@ -34,10 +39,12 @@ SCRATCH = {
     "tF0": ("psum", [128, 512], "float32"),
     "tF1": ("psum", [128, 512], "float32"),
 }
-SEMAPHORES = (["ld", "ldq", "arrQ", "arrA", "arrL", "arrR", "arrP", "sent", "ms", "idn", "st"]
+SEMAPHORES = (["ld", "ldk", "ldv", "ldq", "arrQ", "arrA", "arrLk", "arrLv", "arrRk", "arrRv", "arrP", "sent", "mz", "mk",
+               "ms", "idn", "st"]
               + ["%s%s%d" % (s, p, b) for s in "SREFTCOP" for p in "AL" for b in (0, 1)]
               + ["%sA%d" % (s, b) for s in "UVXWDGH" for b in (0, 1)]
-              + ["%s%d" % (s, b) for s in ("gm", "gw", "gd", "ga", "gr", "gy") for b in (0, 1)])
+              + ["%s%d" % (s, b) for s in ("gm", "gw", "ga", "gr", "gy") for b in (0, 1)]
+              + ["gd%d%d" % (b, j) for b in (0, 1) for j in range(NSLOT)])
 
 
 def _bits(mask):
@@ -59,14 +66,14 @@ def _roles(T, topo):
         for p, h in zip(pd, cand[len(cand) - len(pd):]):
             helper[p] = h
     helpers = [helper[p] for p in ports]
-    locals_ = [c for c in near if c != root and c not in helpers]
-    return root, ports, plain, relay, helper, helpers, locals_
+    givers = [c for c in near if c != root and c not in helpers]
+    return root, ports, plain, relay, helper, helpers, givers
 
 
 def rank_program(g, core, T, topo):
     if T.rank_of(core) is None:
         return
-    root, ports, plain, relay, helper, helpers, locals_ = _roles(T, topo)
+    root, ports, plain, relay, helper, helpers, givers = _roles(T, topo)
     tot = {}
 
     def inc(ins, name, n=1):
@@ -85,27 +92,35 @@ def rank_program(g, core, T, topo):
                      routing_id=rid, dma_engine_mask=m)
         tot["sent"] = tot.get("sent", 0) + _bits(m)
 
-    if core in plain or core in ports:
+    if core in plain:
+        inc(g.sync.dma_start(T.kd[:, :], T.k[:, :]), "ldk", 16)
+        inc(g.scalar.dma_start(T.vd[:, :], T.v[:, :]), "ldv", 16)
+        wait(g, "ldk")
+        send(relay[core], T.rk[:, :], T.kd[:, :], "arrRk")
+        wait(g, "ldv")
+        send(relay[core], T.rv[:, :], T.vd[:, :], "arrRv")
+        wait(g, "sent")
+        return
+    if core in ports:
         inc(g.sync.dma_start(T.kvd[:, 0:128], T.k[:, :]), "ld", 16)
         inc(g.scalar.dma_start(T.kvd[:, 128:256], T.v[:, :]), "ld", 16)
         wait(g, "ld")
-        if core in plain:
-            send(relay[core], T.rly[:, :], T.kvd[:, :], "arrR")
-        else:
-            send(helper[core], T.kvA[:, BW:BW + 256], T.kvd[:, :], "arrA")
-            src = [a for a in plain if relay[a] == core][0]
-            tot["arrR"] = _bits(topo.mask(src, core))
-            wait(g, "arrR")
-            s = plain.index(src)
-            send(root, T.kvL[:, s * BW:s * BW + 256], T.rly[:, :], "arrL")
+        send(helper[core], T.kvA[:, BW:BW + 256], T.kvd[:, :], "arrA")
+        src = [a for a in plain if relay[a] == core][0]
+        s = plain.index(src)
+        tot["arrRk"] = tot["arrRv"] = _bits(topo.mask(src, core))
+        wait(g, "arrRk")
+        send(root, T.kvL[:, s * BW:s * BW + 128], T.rk[:, :], "arrLk")
+        wait(g, "arrRv")
+        send(root, T.kvL[:, s * BW + 128:s * BW + 256], T.rv[:, :], "arrLv")
         wait(g, "sent")
         return
 
-    if core in locals_:
+    if core in givers:
         inc(g.sync.dma_start(T.kvA[:, 0:128], T.k[:, :]), "ld", 16)
         inc(g.scalar.dma_start(T.kvA[:, 128:256], T.v[:, :]), "ld", 16)
         wait(g, "ld")
-        s = 1 + locals_.index(core)
+        s = 1 + givers.index(core)
         send(root, T.kvA[:, s * BW:s * BW + 256], T.kvA[:, 0:256], "arrA")
         wait(g, "sent")
         return
@@ -114,23 +129,26 @@ def rank_program(g, core, T, topo):
     pe, dve, act = g.tensor, g.vector, g.scalar
     sS, tP, oP, tF = [T.sS0, T.sS1], [T.tP0, T.tP1], [T.oP0, T.oP1], [T.tF0, T.tF1]
     Exp = ActivationFunctionType.Exp
-    nA = 1 + len(locals_) if is_root else 2
+    nA = 1 + len(givers) if is_root else 2
 
     if is_root:
         inc(g.sync.dma_start(T.qs[:, :], T.q[:, :]), "ldq", 16)
     inc(g.scalar.dma_start(T.kvA[:, 0:128], T.k[:, :]), "ld", 16)
     inc(g.sync.dma_start(T.kvA[:, 128:256], T.v[:, :]), "ld", 16)
 
-    inc(dve.memset(T.onesb[:, :], 1.0), "ms")
+    inc(dve.memset(T.zero[:, :], 0.0), "mz")
+    wait(g, "mz")
+    inc(g.affine_select(T.msk[:, :], T.zero[:, :], [[-1, 128]], AluOpType.is_equal, -200.0, 0, 1), "mk")
+    wait(act, "mk")
+    inc(act.activation(T.ident[:, :], T.msk[:, :], Exp), "idn")
     for i in range(nA):
         inc(dve.memset(T.kvA[:, i * BW + 256:(i + 1) * BW], 1.0), "ms")
     if is_root:
         for i in range(len(plain)):
             inc(dve.memset(T.kvL[:, i * BW + 256:(i + 1) * BW], 1.0), "ms")
     else:
-        inc(dve.memset(T.msg[:, 260:SW], 0.0), "ms")
-    wait(g, "ms")
-    inc(g.affine_select(T.ident[:, :], T.onesb[:, :], [[-1, 128]], AluOpType.is_equal, 0.0, 0, 1), "idn")
+        for b in (0, 1):
+            inc(dve.memset(T.msg[:, b * HB + 130:(b + 1) * HB], 0.0), "ms")
 
     if is_root:
         wait(g, "ldq")
@@ -141,22 +159,22 @@ def rank_program(g, core, T, topo):
                                               dsts=[T.qs[:, :] for h in helpers], alu_op=0)], local_sem=T.sem.sent)
         tot["sent"] = _bits(m)
         qsem = "ldq"
-        tot["arrA"] = sum(_bits(topo.mask(c, core)) for c in locals_)
-        tot["arrL"] = sum(_bits(topo.mask(relay[a], core)) for a in plain)
+        tot["arrA"] = sum(_bits(topo.mask(c, core)) for c in givers)
+        tot["arrLk"] = tot["arrLv"] = sum(_bits(topo.mask(relay[a], core)) for a in plain)
         tot["arrP"] = sum(_bits(topo.mask(h, core)) for h in helpers)
     else:
         qsem = "arrQ"
         tot["arrQ"] = _bits(topo.mask(root, core))
         tot["arrA"] = _bits(topo.mask([p for p in ports if helper[p] == core][0], core))
 
-    def group(ph, pi, kv, nb, dst, off, data, before, own):
+    def group(ph, pi, kv, nb, dst, off, kdata, vdata, before, own):
         n = nb * 128
         f = 1 if own else 0
         mid = f + (nb - f) // 2
         pieces = [(a, z, s) for a, z, s in ((f, mid, "E"), (mid, nb, "F")) if z > a]
         pT = [T.pT[:, (2 * pi + b) * 512:(2 * pi + b) * 512 + n] for b in (0, 1)]
         pK = [T.pK[:, (2 * pi + b) * 512:(2 * pi + b) * 512 + n] for b in (0, 1)]
-        nm = [dst[:, off + 258 + b:off + 259 + b] for b in (0, 1)]
+        nm = [dst[:, off + b * HB + 129:off + b * HB + 130] for b in (0, 1)]
         nmo = [T.nmo[:, 8 * b:8 * b + 1] for b in (0, 1)]
         qb = [T.qs[:, b * 128:(b + 1) * 128] for b in (0, 1)]
         k = lambda s, b: "%s%s%d" % (s, ph, b)
@@ -172,8 +190,7 @@ def rank_program(g, core, T, topo):
                 wait(act, k("U", b), k("V", b))
                 inc(act.activation(pT[b][:, 0:128], sS[b][:, 0:128], Exp, bias=nmo[b], scale=1.0), k("X", b))
         for b in (0, 1):
-            wait(pe, *data)
-            wait(pe, k("V", b), k("X", b), *old("USVXREF", b))
+            wait(pe, kdata, k("V", b), k("X", b), *old("USVXREF", b))
             for i in range(f, nb):
                 inc(pe.matmul(sS[b][:, i * 128:(i + 1) * 128], qb[b], kv[:, i * BW:i * BW + 128], True, True),
                     k("S", b))
@@ -210,7 +227,7 @@ def rank_program(g, core, T, topo):
             wait(dve, k("T", b))
             inc(dve.tensor_copy(pK[b][:, f * 128:n], tP[b][:, f * 128:n]), k("C", b))
         for b in (0, 1):
-            wait(pe, k("C", b), k("H", b), "ms", *old("OP", b))
+            wait(pe, vdata, k("C", b), k("H", b), "ms", *old("OP", b))
             for i in range(nb):
                 inc(pe.matmul(oP[b][:, 0:129], pK[b][:, i * 128:(i + 1) * 128], kv[:, i * BW + 128:i * BW + 257],
                               i == 0, i == nb - 1), k("O", b))
@@ -218,45 +235,45 @@ def rank_program(g, core, T, topo):
         def evacuate():
             for b in (0, 1):
                 wait(act, k("O", b))
-                inc(act.activation(dst[:, off + b * 129:off + (b + 1) * 129], oP[b][:, 0:129],
+                inc(act.activation(dst[:, off + b * HB:off + b * HB + 129], oP[b][:, 0:129],
                                    ActivationFunctionType.Copy), k("P", b))
         return evacuate
 
     if not is_root:
-        group("A", 0, T.kvA, nA, T.msg, 0, ["arrA"], None, [qsem, "ld"])()
-        wait(g, "RA0", "RA1", "PA0", "PA1")
+        group("A", 0, T.kvA, nA, T.msg, 0, "arrA", "arrA", None, [qsem, "ld"])()
         s = helpers.index(core)
+        wait(g, "ms", "RA0", "RA1", "PA0", "PA1")
         send(root, T.part[:, s * SW:(s + 1) * SW], T.msg[:, :], "arrP")
         wait(g, "sent")
         return
 
     nh = len(helpers)
-    group("A", 0, T.kvA, nA, T.part, nh * SW, ["arrA"], None, [qsem, "ld"])()
-    evac_late = group("L", 1, T.kvL, len(plain), T.part, (nh + 1) * SW, ["arrL"], "A", None)
+    group("A", 0, T.kvA, nA, T.part, nh * SW, "arrA", "arrA", None, [qsem, "ld"])()
+    evac_late = group("L", 1, T.kvL, len(plain), T.part, (nh + 1) * SW, "arrLk", "arrLv", "A", None)
 
-    stat = [T.part[:, 258 + b:258 + b + (NSLOT - 1) * SW + 1:SW] for b in (0, 1)]
+    stat = [T.part[:, b * HB + 129:b * HB + 129 + (NSLOT - 1) * SW + 1:SW] for b in (0, 1)]
+    order = [nh] + list(range(nh)) + [nh + 1]
     for b in (0, 1):
         wait(dve, "arrP", "RA%d" % b, "RL%d" % b)
         inc(dve.tensor_reduce(T.gM[:, 4 * b:4 * b + 1], stat[b], AxisListType.X, AluOpType.min), "gm%d" % b)
-    for b in (0, 1):
         wait(act, "arrP", "RA%d" % b, "RL%d" % b, "gm%d" % b)
         inc(act.activation(T.wj[:, 8 * b:8 * b + NSLOT], stat[b], Exp, bias=T.gM[:, 4 * b:4 * b + 1], scale=-1.0),
             "gw%d" % b)
     evac_late()
     for b in (0, 1):
         wait(dve, "gw%d" % b, "idn")
-        for j in range(NSLOT):
+        for j in order:
             c = (b * NSLOT + j) * 128
             inc(dve.tensor_scalar(T.dg[:, c:c + 128], T.ident[:, :], T.wj[:, 8 * b + j:8 * b + j + 1], None,
-                                  AluOpType.mult), "gd%d" % b)
-    order = [nh] + list(range(nh)) + [nh + 1]
+                                  AluOpType.mult), "gd%d%d" % (b, j))
     for b in (0, 1):
-        wait(pe, "gd%d" % b, "arrP", "PA%d" % b, "SL%d" % b, "RL%d" % b, "EL%d" % b, "FL%d" % b)
+        wait(pe, "arrP", "PA%d" % b, "SL%d" % b, "RL%d" % b, "EL%d" % b, "FL%d" % b)
         for x, j in enumerate(order):
+            wait(pe, "gd%d%d" % (b, j))
             if x == NSLOT - 1:
                 wait(pe, "PL%d" % b)
             c = (b * NSLOT + j) * 128
-            inc(pe.matmul(sS[b][:, 0:129], T.dg[:, c:c + 128], T.part[:, j * SW + b * 129:j * SW + (b + 1) * 129],
+            inc(pe.matmul(sS[b][:, 0:129], T.dg[:, c:c + 128], T.part[:, j * SW + b * HB:j * SW + b * HB + 129],
                           x == 0, x == NSLOT - 1), "ga%d" % b)
     for b in (0, 1):
         wait(dve, "ga%d" % b)
@@ -264,8 +281,8 @@ def rank_program(g, core, T, topo):
         wait(dve, "gr%d" % b)
         inc(dve.tensor_scalar(T.ys[:, b * 128:(b + 1) * 128], sS[b][:, 0:128], T.rc[:, 4 * b:4 * b + 1], None,
                               AluOpType.mult), "gy%d" % b)
-    for b in (0, 1):
-        wait(g.sync, "gy%d" % b)
-        inc(g.sync.dma_start(T.y[b * 128:(b + 1) * 128, :], T.ys[:, b * 128:(b + 1) * 128]), "st", 16)
+    for b, q in ((0, g.sync), (1, act)):
+        wait(q, "gy%d" % b)
+        inc(q.dma_start(T.y[b * 128:(b + 1) * 128, :], T.ys[:, b * 128:(b + 1) * 128]), "st", 16)
     wait(g.sync, "st")
     wait(g, "sent")

@@ -4,7 +4,7 @@ from concourse.mybir import AluOpType, AxisListType, ActivationFunctionType
 BW = 264
 HB = 136
 SW = 2 * HB
-NSLOT = 6
+NSLOT = 7
 
 SCRATCH = {
     "qs": ("sbuf", [128, 256], "bfloat16"),
@@ -22,6 +22,8 @@ SCRATCH = {
     "pK": ("sbuf", [128, 4 * 512], "bfloat16"),
     "part": ("sbuf", [128, NSLOT * SW], "bfloat16"),
     "msg": ("sbuf", [128, SW], "bfloat16"),
+    "sh": ("sbuf", [128, 8], "bfloat16"),
+    "stat": ("sbuf", [128, 8 * NSLOT], "bfloat16"),
     "nmo": ("sbuf", [128, 16], "bfloat16"),
     "wo": ("sbuf", [128, 8], "float32"),
     "dgo": ("sbuf", [128, 256], "bfloat16"),
@@ -39,8 +41,8 @@ SCRATCH = {
     "tF0": ("psum", [128, 512], "float32"),
     "tF1": ("psum", [128, 512], "float32"),
 }
-SEMAPHORES = (["ld", "ldk", "ldv", "ldq", "arrQ", "arrA", "arrLk", "arrLv", "arrRk", "arrRv", "arrP", "sent", "mz", "mk",
-               "ms", "idn", "st"]
+SEMAPHORES = (["ld", "ldk", "ldv", "ldq", "arrQ", "arrA", "arrLk", "arrLv", "arrRk", "arrRv", "arrP", "arrG", "arrM",
+               "sent", "mz", "mk", "ms", "idn", "st"]
               + ["%s%s%d" % (s, p, b) for s in "SREFTCOP" for p in "AL" for b in (0, 1)]
               + ["%sA%d" % (s, b) for s in "UVXWDGH" for b in (0, 1)]
               + ["%s%d" % (s, b) for s in ("gm", "gw", "ga", "gr", "gy") for b in (0, 1)]
@@ -66,14 +68,16 @@ def _roles(T, topo):
         for p, h in zip(pd, cand[len(cand) - len(pd):]):
             helper[p] = h
     helpers = [helper[p] for p in ports]
-    givers = [c for c in near if c != root and c not in helpers]
-    return root, ports, plain, relay, helper, helpers, givers
+    spare = [c for c in near if c != root and c not in helpers]
+    fifth = ([c for c in spare if topo.die(c) == topo.die(root)] or spare)[0]
+    givers = [c for c in spare if c != fifth]
+    return root, ports, plain, relay, helper, helpers, fifth, givers
 
 
 def rank_program(g, core, T, topo):
     if T.rank_of(core) is None:
         return
-    root, ports, plain, relay, helper, helpers, givers = _roles(T, topo)
+    root, ports, plain, relay, helper, helpers, fifth, givers = _roles(T, topo)
     tot = {}
 
     def inc(ins, name, n=1):
@@ -121,7 +125,7 @@ def rank_program(g, core, T, topo):
         inc(g.scalar.dma_start(T.kvA[:, 128:256], T.v[:, :]), "ld", 16)
         wait(g, "ld")
         s = 1 + givers.index(core)
-        send(root, T.kvA[:, s * BW:s * BW + 256], T.kvA[:, 0:256], "arrA")
+        send(fifth, T.kvA[:, s * BW:s * BW + 256], T.kvA[:, 0:256], "arrA")
         wait(g, "sent")
         return
 
@@ -129,7 +133,8 @@ def rank_program(g, core, T, topo):
     pe, dve, act = g.tensor, g.vector, g.scalar
     sS, tP, oP, tF = [T.sS0, T.sS1], [T.tP0, T.tP1], [T.oP0, T.oP1], [T.tF0, T.tF1]
     Exp = ActivationFunctionType.Exp
-    nA = 1 + len(givers) if is_root else 2
+    nA = 1 if is_root else 1 + len(givers) if core == fifth else 2
+    hs = helpers + [fifth]
 
     if is_root:
         inc(g.sync.dma_start(T.qs[:, :], T.q[:, :]), "ldq", 16)
@@ -148,7 +153,8 @@ def rank_program(g, core, T, topo):
             inc(dve.memset(T.kvL[:, i * BW + 256:(i + 1) * BW], 1.0), "ms")
     else:
         for b in (0, 1):
-            inc(dve.memset(T.msg[:, b * HB + 130:(b + 1) * HB], 0.0), "ms")
+            inc(dve.memset(T.msg[:, b * HB + 129:(b + 1) * HB], 0.0), "ms")
+        inc(dve.memset(T.sh[:, 2:8], 0.0), "ms")
 
     if is_root:
         wait(g, "ldq")
@@ -158,23 +164,26 @@ def rank_program(g, core, T, topo):
                                               remote_sem=T.sem.arrQ, srcs=[T.qs[:, :]],
                                               dsts=[T.qs[:, :] for h in helpers], alu_op=0)], local_sem=T.sem.sent)
         tot["sent"] = _bits(m)
+        send(fifth, T.qs[:, :], T.qs[:, :], "arrQ")
         qsem = "ldq"
-        tot["arrA"] = sum(_bits(topo.mask(c, core)) for c in givers)
         tot["arrLk"] = tot["arrLv"] = sum(_bits(topo.mask(relay[a], core)) for a in plain)
         tot["arrP"] = sum(_bits(topo.mask(h, core)) for h in helpers)
+        tot["arrG"] = _bits(topo.mask(fifth, core))
+        tot["arrM"] = tot["arrP"] + tot["arrG"]
     else:
         qsem = "arrQ"
         tot["arrQ"] = _bits(topo.mask(root, core))
-        tot["arrA"] = _bits(topo.mask([p for p in ports if helper[p] == core][0], core))
+        tot["arrA"] = sum(_bits(topo.mask(c, core)) for c in (givers if core == fifth else
+                                                              [p for p in ports if helper[p] == core]))
 
-    def group(ph, pi, kv, nb, dst, off, kdata, vdata, before, own):
+    def group(ph, pi, kv, nb, dst, off, sh, so, kdata, vdata, before, own):
         n = nb * 128
         f = 1 if own else 0
         mid = f + (nb - f) // 2
         pieces = [(a, z, s) for a, z, s in ((f, mid, "E"), (mid, nb, "F")) if z > a]
         pT = [T.pT[:, (2 * pi + b) * 512:(2 * pi + b) * 512 + n] for b in (0, 1)]
         pK = [T.pK[:, (2 * pi + b) * 512:(2 * pi + b) * 512 + n] for b in (0, 1)]
-        nm = [dst[:, off + b * HB + 129:off + b * HB + 130] for b in (0, 1)]
+        nm = [sh[:, so + b:so + b + 1] for b in (0, 1)]
         nmo = [T.nmo[:, 8 * b:8 * b + 1] for b in (0, 1)]
         qb = [T.qs[:, b * 128:(b + 1) * 128] for b in (0, 1)]
         k = lambda s, b: "%s%s%d" % (s, ph, b)
@@ -190,7 +199,8 @@ def rank_program(g, core, T, topo):
                 wait(act, k("U", b), k("V", b))
                 inc(act.activation(pT[b][:, 0:128], sS[b][:, 0:128], Exp, bias=nmo[b], scale=1.0), k("X", b))
         for b in (0, 1):
-            wait(pe, kdata, k("V", b), k("X", b), *old("USVXREF", b))
+            wait(pe, *kdata)
+            wait(pe, k("V", b), k("X", b), *old("USVXREF", b))
             for i in range(f, nb):
                 inc(pe.matmul(sS[b][:, i * 128:(i + 1) * 128], qb[b], kv[:, i * BW:i * BW + 128], True, True),
                     k("S", b))
@@ -227,7 +237,8 @@ def rank_program(g, core, T, topo):
             wait(dve, k("T", b))
             inc(dve.tensor_copy(pK[b][:, f * 128:n], tP[b][:, f * 128:n]), k("C", b))
         for b in (0, 1):
-            wait(pe, vdata, k("C", b), k("H", b), "ms", *old("OP", b))
+            wait(pe, *vdata)
+            wait(pe, k("C", b), k("H", b), "ms", *old("OP", b))
             for i in range(nb):
                 inc(pe.matmul(oP[b][:, 0:129], pK[b][:, i * 128:(i + 1) * 128], kv[:, i * BW + 128:i * BW + 257],
                               i == 0, i == nb - 1), k("O", b))
@@ -240,23 +251,26 @@ def rank_program(g, core, T, topo):
         return evacuate
 
     if not is_root:
-        group("A", 0, T.kvA, nA, T.msg, 0, "arrA", "arrA", None, [qsem, "ld"])()
-        s = helpers.index(core)
-        wait(g, "ms", "RA0", "RA1", "PA0", "PA1")
-        send(root, T.part[:, s * SW:(s + 1) * SW], T.msg[:, :], "arrP")
+        group("A", 0, T.kvA, nA, T.msg, 0, T.sh, 0, ["arrA"], ["arrA"], None, [qsem, "ld"])()
+        s = hs.index(core)
+        wait(g, "ms", "RA0", "RA1")
+        send(root, T.stat[:, s * 8:(s + 1) * 8], T.sh[:, :], "arrM")
+        wait(g, "PA0", "PA1")
+        send(root, T.part[:, s * SW:(s + 1) * SW], T.msg[:, :], "arrG" if core == fifth else "arrP")
         wait(g, "sent")
         return
 
-    nh = len(helpers)
-    group("A", 0, T.kvA, nA, T.part, nh * SW, "arrA", "arrA", None, [qsem, "ld"])()
-    evac_late = group("L", 1, T.kvL, len(plain), T.part, (nh + 1) * SW, "arrLk", "arrLv", "A", None)
+    nh = len(hs)
+    sA, sL = nh, nh + 1
+    group("A", 0, T.kvA, nA, T.part, sA * SW, T.stat, sA * 8, [qsem, "ld"], ["ld"], None, None)()
+    evac_late = group("L", 1, T.kvL, len(plain), T.part, sL * SW, T.stat, sL * 8, ["arrLk"], ["arrLv"], "A", None)
 
-    stat = [T.part[:, b * HB + 129:b * HB + 129 + (NSLOT - 1) * SW + 1:SW] for b in (0, 1)]
-    order = [nh] + list(range(nh)) + [nh + 1]
+    stat = [T.stat[:, b:b + (NSLOT - 1) * 8 + 1:8] for b in (0, 1)]
+    order = [sA] + list(range(len(helpers))) + [sL, nh - 1]
     for b in (0, 1):
-        wait(dve, "arrP", "RA%d" % b, "RL%d" % b)
+        wait(dve, "arrM", "RA%d" % b, "RL%d" % b)
         inc(dve.tensor_reduce(T.gM[:, 4 * b:4 * b + 1], stat[b], AxisListType.X, AluOpType.min), "gm%d" % b)
-        wait(act, "arrP", "RA%d" % b, "RL%d" % b, "gm%d" % b)
+        wait(act, "arrM", "RA%d" % b, "RL%d" % b, "gm%d" % b)
         inc(act.activation(T.wj[:, 8 * b:8 * b + NSLOT], stat[b], Exp, bias=T.gM[:, 4 * b:4 * b + 1], scale=-1.0),
             "gw%d" % b)
     evac_late()
@@ -267,11 +281,10 @@ def rank_program(g, core, T, topo):
             inc(dve.tensor_scalar(T.dg[:, c:c + 128], T.ident[:, :], T.wj[:, 8 * b + j:8 * b + j + 1], None,
                                   AluOpType.mult), "gd%d%d" % (b, j))
     for b in (0, 1):
-        wait(pe, "arrP", "PA%d" % b, "SL%d" % b, "RL%d" % b, "EL%d" % b, "FL%d" % b)
+        wait(pe, "PA%d" % b, "SL%d" % b, "RL%d" % b, "EL%d" % b, "FL%d" % b)
         for x, j in enumerate(order):
             wait(pe, "gd%d%d" % (b, j))
-            if x == NSLOT - 1:
-                wait(pe, "PL%d" % b)
+            wait(pe, "PL%d" % b if j == sL else "arrG" if j == nh - 1 else "arrP" if j < nh else "PA%d" % b)
             c = (b * NSLOT + j) * 128
             inc(pe.matmul(sS[b][:, 0:129], T.dg[:, c:c + 128], T.part[:, j * SW + b * HB:j * SW + b * HB + 129],
                           x == 0, x == NSLOT - 1), "ga%d" % b)

@@ -4,7 +4,9 @@ from concourse.mybir import AluOpType, AxisListType, ActivationFunctionType
 BW = 264
 HB = 136
 SW = 2 * HB
-NSLOT = 7
+NP = 6
+NSLOT = NP + 1
+CLAMP = 20.0
 
 SCRATCH = {
     "qs": ("sbuf", [128, 256], "bfloat16"),
@@ -20,7 +22,7 @@ SCRATCH = {
     "ident": ("sbuf", [128, 128], "bfloat16"),
     "pT": ("sbuf", [128, 4 * 512], "bfloat16"),
     "pK": ("sbuf", [128, 4 * 512], "bfloat16"),
-    "part": ("sbuf", [128, NSLOT * SW], "bfloat16"),
+    "part": ("sbuf", [128, NP * SW], "bfloat16"),
     "msg": ("sbuf", [128, SW], "bfloat16"),
     "sh": ("sbuf", [128, 8], "bfloat16"),
     "stat": ("sbuf", [128, 8 * NSLOT], "bfloat16"),
@@ -28,9 +30,12 @@ SCRATCH = {
     "wo": ("sbuf", [128, 8], "float32"),
     "dgo": ("sbuf", [128, 256], "bfloat16"),
     "gM": ("sbuf", [128, 8], "float32"),
+    "gB": ("sbuf", [128, 8], "float32"),
     "wj": ("sbuf", [128, 16], "float32"),
-    "rc": ("sbuf", [128, 8], "float32"),
-    "dg": ("sbuf", [128, 2 * NSLOT * 128], "bfloat16"),
+    "lw": ("sbuf", [128, 16], "float32"),
+    "lt": ("sbuf", [128, 4], "float32"),
+    "rc": ("sbuf", [128, 4], "float32"),
+    "dg": ("sbuf", [128, 2 * NP * 128], "bfloat16"),
     "ys": ("sbuf", [128, 256], "bfloat16"),
     "sS0": ("psum", [128, 512], "float32"),
     "sS1": ("psum", [128, 512], "float32"),
@@ -41,12 +46,13 @@ SCRATCH = {
     "tF0": ("psum", [128, 512], "float32"),
     "tF1": ("psum", [128, 512], "float32"),
 }
-SEMAPHORES = (["ld", "ldk", "ldv", "ldq", "arrQ", "arrA", "arrLk", "arrLv", "arrRk", "arrRv", "arrP", "arrG", "arrM",
-               "sent", "mz", "mk", "ms", "idn", "st"]
+SEMAPHORES = (["ld", "ldk", "ldv", "ldq", "arrQ", "arrA", "arrLk", "arrLv", "arrRk", "arrRv", "arrM",
+               "sent", "mz", "mk", "ms", "idn", "st", "gr"]
+              + ["aP%d" % j for j in range(NP - 1)]
               + ["%s%s%d" % (s, p, b) for s in "SREFTCOP" for p in "AL" for b in (0, 1)]
               + ["%sA%d" % (s, b) for s in "UVXWDGH" for b in (0, 1)]
-              + ["%s%d" % (s, b) for s in ("gm", "gw", "ga", "gr", "gy") for b in (0, 1)]
-              + ["gd%d%d" % (b, j) for b in (0, 1) for j in range(NSLOT)])
+              + ["%s%d" % (s, b) for s in ("gm", "gb", "gw", "ga", "la", "lr", "gy") for b in (0, 1)]
+              + ["gd%d%d" % (b, j) for b in (0, 1) for j in range(NP)])
 
 
 def _bits(mask):
@@ -132,7 +138,7 @@ def rank_program(g, core, T, topo):
     is_root = core == root
     pe, dve, act = g.tensor, g.vector, g.scalar
     sS, tP, oP, tF = [T.sS0, T.sS1], [T.tP0, T.tP1], [T.oP0, T.oP1], [T.tF0, T.tF1]
-    Exp = ActivationFunctionType.Exp
+    Exp, Copy = ActivationFunctionType.Exp, ActivationFunctionType.Copy
     nA = 1 if is_root else 1 + len(givers) if core == fifth else 2
     hs = helpers + [fifth]
 
@@ -167,16 +173,16 @@ def rank_program(g, core, T, topo):
         send(fifth, T.qs[:, :], T.qs[:, :], "arrQ")
         qsem = "ldq"
         tot["arrLk"] = tot["arrLv"] = sum(_bits(topo.mask(relay[a], core)) for a in plain)
-        tot["arrP"] = sum(_bits(topo.mask(h, core)) for h in helpers)
-        tot["arrG"] = _bits(topo.mask(fifth, core))
-        tot["arrM"] = tot["arrP"] + tot["arrG"]
+        for j, h in enumerate(hs):
+            tot["aP%d" % j] = _bits(topo.mask(h, core))
+        tot["arrM"] = sum(_bits(topo.mask(h, core)) for h in hs)
     else:
         qsem = "arrQ"
         tot["arrQ"] = _bits(topo.mask(root, core))
         tot["arrA"] = sum(_bits(topo.mask(c, core)) for c in (givers if core == fifth else
                                                               [p for p in ports if helper[p] == core]))
 
-    def group(ph, pi, kv, nb, dst, off, sh, so, kdata, vdata, before, own):
+    def group(ph, pi, kv, nb, dst, off, sh, so, kdata, vdata, before, own, keep=False):
         n = nb * 128
         f = 1 if own else 0
         mid = f + (nb - f) // 2
@@ -211,9 +217,9 @@ def rank_program(g, core, T, topo):
             wait(act, k("S", b), k("R", b))
             if own:
                 inc(act.activation(T.wo[:, 4 * b:4 * b + 1], nmo[b], Exp, bias=nm[b], scale=-1.0), k("W", b))
-            for a, z, s in pieces:
-                inc(act.activation(pT[b][:, a * 128:z * 128], sS[b][:, a * 128:z * 128], Exp, bias=nm[b], scale=1.0),
-                    k(s, b))
+            for x, (a, z, s) in enumerate(pieces):
+                inc(act.activation(pT[b][:, a * 128:z * 128], sS[b][:, a * 128:z * 128], Exp, bias=nm[b], scale=1.0,
+                                   accum_out=T.lw[:, 8 * b + NP + x:8 * b + NP + x + 1] if keep else None), k(s, b))
         if own:
             for b in (0, 1):
                 wait(dve, k("W", b), "idn")
@@ -241,59 +247,67 @@ def rank_program(g, core, T, topo):
             wait(pe, k("C", b), k("H", b), "ms", *old("OP", b))
             for i in range(nb):
                 inc(pe.matmul(oP[b][:, 0:129], pK[b][:, i * 128:(i + 1) * 128], kv[:, i * BW + 128:i * BW + 257],
-                              i == 0, i == nb - 1), k("O", b))
-
-        def evacuate():
-            for b in (0, 1):
-                wait(act, k("O", b))
-                inc(act.activation(dst[:, off + b * HB:off + b * HB + 129], oP[b][:, 0:129],
-                                   ActivationFunctionType.Copy), k("P", b))
-        return evacuate
+                              i == 0, i == nb - 1 and not keep), k("O", b))
+        if keep:
+            return
+        for b in (0, 1):
+            wait(act, k("O", b))
+            inc(act.activation(dst[:, off + b * HB:off + b * HB + 129], oP[b][:, 0:129], Copy), k("P", b))
 
     if not is_root:
-        group("A", 0, T.kvA, nA, T.msg, 0, T.sh, 0, ["arrA"], ["arrA"], None, [qsem, "ld"])()
+        group("A", 0, T.kvA, nA, T.msg, 0, T.sh, 0, ["arrA"], ["arrA"], None, [qsem, "ld"])
         s = hs.index(core)
         wait(g, "ms", "RA0", "RA1")
         send(root, T.stat[:, s * 8:(s + 1) * 8], T.sh[:, :], "arrM")
         wait(g, "PA0", "PA1")
-        send(root, T.part[:, s * SW:(s + 1) * SW], T.msg[:, :], "arrG" if core == fifth else "arrP")
+        send(root, T.part[:, s * SW:(s + 1) * SW], T.msg[:, :], "aP%d" % s)
         wait(g, "sent")
         return
 
     nh = len(hs)
     sA, sL = nh, nh + 1
-    group("A", 0, T.kvA, nA, T.part, sA * SW, T.stat, sA * 8, [qsem, "ld"], ["ld"], None, None)()
-    evac_late = group("L", 1, T.kvL, len(plain), T.part, sL * SW, T.stat, sL * 8, ["arrLk"], ["arrLv"], "A", None)
+    group("A", 0, T.kvA, nA, T.part, sA * SW, T.stat, sA * 8, [qsem, "ld"], ["ld"], None, None)
+    group("L", 1, T.kvL, len(plain), None, 0, T.stat, sL * 8, ["arrLk"], ["arrLv"], "A", None, keep=True)
 
-    stat = [T.stat[:, b:b + (NSLOT - 1) * 8 + 1:8] for b in (0, 1)]
-    order = [sA] + list(range(len(helpers))) + [sL, nh - 1]
+    order = [sA] + list(range(nh))
     for b in (0, 1):
         wait(dve, "arrM", "RA%d" % b, "RL%d" % b)
-        inc(dve.tensor_reduce(T.gM[:, 4 * b:4 * b + 1], stat[b], AxisListType.X, AluOpType.min), "gm%d" % b)
-        wait(act, "arrM", "RA%d" % b, "RL%d" % b, "gm%d" % b)
-        inc(act.activation(T.wj[:, 8 * b:8 * b + NSLOT], stat[b], Exp, bias=T.gM[:, 4 * b:4 * b + 1], scale=-1.0),
-            "gw%d" % b)
-    evac_late()
+        inc(dve.tensor_reduce(T.gM[:, 4 * b:4 * b + 1], T.stat[:, b:b + (NSLOT - 1) * 8 + 1:8], AxisListType.X,
+                              AluOpType.min), "gm%d" % b)
     for b in (0, 1):
-        wait(dve, "gw%d" % b, "idn")
-        for j in order:
-            c = (b * NSLOT + j) * 128
-            inc(dve.tensor_scalar(T.dg[:, c:c + 128], T.ident[:, :], T.wj[:, 8 * b + j:8 * b + j + 1], None,
-                                  AluOpType.mult), "gd%d%d" % (b, j))
+        wait(dve, "gm%d" % b)
+        inc(dve.tensor_scalar(T.gB[:, 4 * b:4 * b + 1], T.gM[:, 4 * b:4 * b + 1], CLAMP,
+                              T.stat[:, sL * 8 + b:sL * 8 + b + 1], AluOpType.add, AluOpType.min), "gb%d" % b)
+        wait(act, "arrM", "RA%d" % b, "gb%d" % b)
+        inc(act.activation(T.wj[:, 8 * b:8 * b + NP], T.stat[:, b:b + (NP - 1) * 8 + 1:8], Exp,
+                           bias=T.gB[:, 4 * b:4 * b + 1], scale=-1.0), "gw%d" % b)
+    wait(dve, "gw0", "idn")
+    wait(act, "gw1", "idn")
+    for j in order:
+        c0, c1 = j * 128, (NP + j) * 128
+        inc(dve.tensor_scalar(T.dg[:, c0:c0 + 128], T.ident[:, :], T.wj[:, j:j + 1], None, AluOpType.mult),
+            "gd0%d" % j)
+        inc(act.activation(T.dg[:, c1:c1 + 128], T.ident[:, :], Copy, scale=T.wj[:, 8 + j:8 + j + 1]), "gd1%d" % j)
+    for x, j in enumerate(order):
+        for b in (0, 1):
+            wait(pe, "gd%d%d" % (b, j), "aP%d" % j if j < nh else "PA%d" % b)
+            c = (b * NP + j) * 128
+            inc(pe.matmul(oP[b][:, 0:129], T.dg[:, c:c + 128], T.part[:, j * SW + b * HB:j * SW + b * HB + 129],
+                          False, x == NP - 1), "ga%d" % b)
     for b in (0, 1):
-        wait(pe, "PA%d" % b, "SL%d" % b, "RL%d" % b, "EL%d" % b, "FL%d" % b)
-        for x, j in enumerate(order):
-            wait(pe, "gd%d%d" % (b, j))
-            wait(pe, "PL%d" % b if j == sL else "arrG" if j == nh - 1 else "arrP" if j < nh else "PA%d" % b)
-            c = (b * NSLOT + j) * 128
-            inc(pe.matmul(sS[b][:, 0:129], T.dg[:, c:c + 128], T.part[:, j * SW + b * HB:j * SW + b * HB + 129],
-                          x == 0, x == NSLOT - 1), "ga%d" % b)
+        wait(dve, "PA%d" % b, "gw%d" % b, *["aP%d" % j for j in range(nh)])
+        inc(dve.tensor_tensor(T.lw[:, 8 * b:8 * b + NP], T.wj[:, 8 * b:8 * b + NP],
+                              T.part[:, b * HB + 128:b * HB + 128 + (NP - 1) * SW + 1:SW], AluOpType.mult), "la%d" % b)
     for b in (0, 1):
-        wait(dve, "ga%d" % b)
-        inc(dve.reciprocal(T.rc[:, 4 * b:4 * b + 1], sS[b][:, 128:129]), "gr%d" % b)
-        wait(dve, "gr%d" % b)
-        inc(dve.tensor_scalar(T.ys[:, b * 128:(b + 1) * 128], sS[b][:, 0:128], T.rc[:, 4 * b:4 * b + 1], None,
-                              AluOpType.mult), "gy%d" % b)
+        wait(dve, "la%d" % b, "EL%d" % b, "FL%d" % b)
+        inc(dve.tensor_reduce(T.lt[:, b:b + 1], T.lw[:, 8 * b:8 * b + NP + 2], AxisListType.X, AluOpType.add),
+            "lr%d" % b)
+    wait(dve, "lr0", "lr1")
+    inc(dve.reciprocal(T.rc[:, 0:2], T.lt[:, 0:2]), "gr")
+    wait(dve, "OL0", "ga0", "gr")
+    inc(dve.tensor_scalar(T.ys[:, 0:128], oP[0][:, 0:128], T.rc[:, 0:1], None, AluOpType.mult), "gy0")
+    wait(act, "OL1", "ga1", "gr")
+    inc(act.activation(T.ys[:, 128:256], oP[1][:, 0:128], Copy, scale=T.rc[:, 1:2]), "gy1")
     for b, q in ((0, g.sync), (1, act)):
         wait(q, "gy%d" % b)
         inc(q.dma_start(T.y[b * 128:(b + 1) * 128, :], T.ys[:, b * 128:(b + 1) * 128]), "st", 16)

from concourse.bass import DstId, RemoteDMATransfer
from concourse.mybir import AluOpType, AxisListType, ActivationFunctionType

BW = 264
HB = 136
SW = 2 * HB
NP = 6
NSLOT = NP + 1
CLAMP = 20.0

SCRATCH = {
    "qs": ("sbuf", [128, 256], "bfloat16"),
    "kvd": ("dram", [128, 256], "bfloat16"),
    "kd": ("dram", [128, 128], "bfloat16"),
    "vd": ("dram", [128, 128], "bfloat16"),
    "rk": ("dram", [128, 128], "bfloat16"),
    "rv": ("dram", [128, 128], "bfloat16"),
    "kvA": ("sbuf", [128, 4 * BW], "bfloat16"),
    "kvL": ("sbuf", [128, 4 * BW], "bfloat16"),
    "zero": ("sbuf", [128, 128], "bfloat16"),
    "msk": ("sbuf", [128, 128], "bfloat16"),
    "ident": ("sbuf", [128, 128], "bfloat16"),
    "pT": ("sbuf", [128, 4 * 512], "bfloat16"),
    "pK": ("sbuf", [128, 4 * 512], "bfloat16"),
    "part": ("sbuf", [128, NP * SW], "bfloat16"),
    "msg": ("sbuf", [128, SW], "bfloat16"),
    "sh": ("sbuf", [128, 8], "bfloat16"),
    "stat": ("sbuf", [128, 8 * NSLOT], "bfloat16"),
    "nmo": ("sbuf", [128, 16], "bfloat16"),
    "wo": ("sbuf", [128, 8], "float32"),
    "dgo": ("sbuf", [128, 256], "bfloat16"),
    "gM": ("sbuf", [128, 8], "float32"),
    "gB": ("sbuf", [128, 8], "float32"),
    "wj": ("sbuf", [128, 16], "float32"),
    "lw": ("sbuf", [128, 16], "float32"),
    "lt": ("sbuf", [128, 4], "float32"),
    "rc": ("sbuf", [128, 4], "float32"),
    "dg": ("sbuf", [128, 2 * NP * 128], "bfloat16"),
    "ys": ("sbuf", [128, 256], "bfloat16"),
    "sS0": ("psum", [128, 512], "float32"),
    "sS1": ("psum", [128, 512], "float32"),
    "tP0": ("psum", [128, 1024], "bfloat16"),
    "tP1": ("psum", [128, 1024], "bfloat16"),
    "oP0": ("psum", [128, 512], "float32"),
    "oP1": ("psum", [128, 512], "float32"),
    "tF0": ("psum", [128, 512], "float32"),
    "tF1": ("psum", [128, 512], "float32"),
}
SEMAPHORES = (["ld", "ldk", "ldv", "ldq", "arrQ", "arrA", "arrLk", "arrLv", "arrRk", "arrRv", "arrM",
               "sent", "mz", "mk", "ms", "idn", "st", "gr"]
              + ["aP%d" % j for j in range(NP - 1)]
              + ["%s%s%d" % (s, p, b) for s in "SREFTCOP" for p in "AL" for b in (0, 1)]
              + ["%sA%d" % (s, b) for s in "UVXWDGH" for b in (0, 1)]
              + ["%s%d" % (s, b) for s in ("gm", "gb", "gw", "ga", "la", "lr", "gy") for b in (0, 1)]
              + ["gd%d%d" % (b, j) for b in (0, 1) for j in range(NP)])


def _bits(mask):
    return bin(mask).count("1")


def _roles(T, topo):
    root = T.cores[T.root]
    near = [c for c in T.cores if topo.host(c) == topo.host(root) and topo.chip(c) == topo.chip(root)]
    far = [c for c in T.cores if c not in near]
    ports = [c for c in far if topo.may_write(c, root)]
    plain = [c for c in far if c not in ports]
    relay, helper = {}, {}
    for d in sorted(set(topo.die(c) for c in far)):
        pd = [c for c in ports if topo.die(c) == d]
        for a, p in zip([c for c in plain if topo.die(c) == d], pd):
            relay[a] = p
        cand = [c for c in near if c != root and topo.die(c) == d]
        for p, h in zip(pd, cand[len(cand) - len(pd):]):
            helper[p] = h
    helpers = [helper[p] for p in ports]
    spare = [c for c in near if c != root and c not in helpers]
    fifth = ([c for c in spare if topo.die(c) == topo.die(root)] or spare)[0]
    givers = [c for c in spare if c != fifth]
    return root, ports, plain, relay, helper, helpers, fifth, givers


def rank_program(g, core, T, topo):
    if T.rank_of(core) is None:
        return
    root, ports, plain, relay, helper, helpers, fifth, givers = _roles(T, topo)
    tot = {}

    def inc(ins, name, n=1):
        ins.then_inc(T.sem[name], n)
        tot[name] = tot.get(name, 0) + n

    def wait(q, *names):
        for name in names:
            if name in tot:
                q.wait_ge(T.sem[name], tot[name])

    def send(dst, out_ap, in_ap, rsem):
        rid, pid = topo.addr(dst, core)
        m = topo.mask(core, dst)
        g.remote_dma(out_ap=out_ap, in_ap=in_ap, remote_sem=T.sem[rsem], local_sem=T.sem.sent, pid=pid,
                     routing_id=rid, dma_engine_mask=m)
        tot["sent"] = tot.get("sent", 0) + _bits(m)

    if core in plain:
        inc(g.sync.dma_start(T.kd[:, :], T.k[:, :]), "ldk", 16)
        inc(g.scalar.dma_start(T.vd[:, :], T.v[:, :]), "ldv", 16)
        wait(g, "ldk")
        send(relay[core], T.rk[:, :], T.kd[:, :], "arrRk")
        wait(g, "ldv")
        send(relay[core], T.rv[:, :], T.vd[:, :], "arrRv")
        wait(g, "sent")
        return
    if core in ports:
        inc(g.sync.dma_start(T.kvd[:, 0:128], T.k[:, :]), "ld", 16)
        inc(g.scalar.dma_start(T.kvd[:, 128:256], T.v[:, :]), "ld", 16)
        wait(g, "ld")
        send(helper[core], T.kvA[:, BW:BW + 256], T.kvd[:, :], "arrA")
        src = [a for a in plain if relay[a] == core][0]
        s = plain.index(src)
        tot["arrRk"] = tot["arrRv"] = _bits(topo.mask(src, core))
        wait(g, "arrRk")
        send(root, T.kvL[:, s * BW:s * BW + 128], T.rk[:, :], "arrLk")
        wait(g, "arrRv")
        send(root, T.kvL[:, s * BW + 128:s * BW + 256], T.rv[:, :], "arrLv")
        wait(g, "sent")
        return

    if core in givers:
        inc(g.sync.dma_start(T.kvA[:, 0:128], T.k[:, :]), "ld", 16)
        inc(g.scalar.dma_start(T.kvA[:, 128:256], T.v[:, :]), "ld", 16)
        wait(g, "ld")
        s = 1 + givers.index(core)
        send(fifth, T.kvA[:, s * BW:s * BW + 256], T.kvA[:, 0:256], "arrA")
        wait(g, "sent")
        return

    is_root = core == root
    pe, dve, act = g.tensor, g.vector, g.scalar
    sS, tP, oP, tF = [T.sS0, T.sS1], [T.tP0, T.tP1], [T.oP0, T.oP1], [T.tF0, T.tF1]
    Exp, Copy = ActivationFunctionType.Exp, ActivationFunctionType.Copy
    nA = 1 if is_root else 1 + len(givers) if core == fifth else 2
    hs = helpers + [fifth]

    if is_root:
        inc(g.sync.dma_start(T.qs[:, :], T.q[:, :]), "ldq", 16)
    inc(g.scalar.dma_start(T.kvA[:, 0:128], T.k[:, :]), "ld", 16)
    inc(g.sync.dma_start(T.kvA[:, 128:256], T.v[:, :]), "ld", 16)

    inc(dve.memset(T.zero[:, :], 0.0), "mz")
    wait(g, "mz")
    inc(g.affine_select(T.msk[:, :], T.zero[:, :], [[-1, 128]], AluOpType.is_equal, -200.0, 0, 1), "mk")
    wait(act, "mk")
    inc(act.activation(T.ident[:, :], T.msk[:, :], Exp), "idn")
    for i in range(nA):
        inc(dve.memset(T.kvA[:, i * BW + 256:(i + 1) * BW], 1.0), "ms")
    if is_root:
        for i in range(len(plain)):
            inc(dve.memset(T.kvL[:, i * BW + 256:(i + 1) * BW], 1.0), "ms")
    else:
        for b in (0, 1):
            inc(dve.memset(T.msg[:, b * HB + 129:(b + 1) * HB], 0.0), "ms")
        inc(dve.memset(T.sh[:, 2:8], 0.0), "ms")

    if is_root:
        wait(g, "ldq")
        m = topo.mask(core, helpers[0])
        ids = [topo.addr(h, core) for h in helpers]
        g.remote_dma_fused([RemoteDMATransfer(dst_ids=[DstId(rid=r, pnc=p) for r, p in ids], dma_engine_mask=m,
                                              remote_sem=T.sem.arrQ, srcs=[T.qs[:, :]],
                                              dsts=[T.qs[:, :] for h in helpers], alu_op=0)], local_sem=T.sem.sent)
        tot["sent"] = _bits(m)
        send(fifth, T.qs[:, :], T.qs[:, :], "arrQ")
        qsem = "ldq"
        tot["arrLk"] = tot["arrLv"] = sum(_bits(topo.mask(relay[a], core)) for a in plain)
        for j, h in enumerate(hs):
            tot["aP%d" % j] = _bits(topo.mask(h, core))
        tot["arrM"] = sum(_bits(topo.mask(h, core)) for h in hs)
    else:
        qsem = "arrQ"
        tot["arrQ"] = _bits(topo.mask(root, core))
        tot["arrA"] = sum(_bits(topo.mask(c, core)) for c in (givers if core == fifth else
                                                              [p for p in ports if helper[p] == core]))

    def group(ph, pi, kv, nb, dst, off, sh, so, kdata, vdata, before, own, keep=False):
        n = nb * 128
        f = 1 if own else 0
        mid = f + (nb - f) // 2
        pieces = [(a, z, s) for a, z, s in ((f, mid, "E"), (mid, nb, "F")) if z > a]
        pT = [T.pT[:, (2 * pi + b) * 512:(2 * pi + b) * 512 + n] for b in (0, 1)]
        pK = [T.pK[:, (2 * pi + b) * 512:(2 * pi + b) * 512 + n] for b in (0, 1)]
        nm = [sh[:, so + b:so + b + 1] for b in (0, 1)]
        nmo = [T.nmo[:, 8 * b:8 * b + 1] for b in (0, 1)]
        qb = [T.qs[:, b * 128:(b + 1) * 128] for b in (0, 1)]
        k = lambda s, b: "%s%s%d" % (s, ph, b)
        old = lambda ss, b: ["%s%s%d" % (s, before, b) for s in ss] if before else []
        if own:
            for b in (0, 1):
                wait(pe, *own)
                inc(pe.matmul(sS[b][:, 0:128], qb[b], kv[:, 0:128], True, True), k("U", b))
            for b in (0, 1):
                wait(dve, k("U", b))
                inc(dve.tensor_reduce(nmo[b], sS[b][:, 0:128], AxisListType.X, AluOpType.max, negate=True), k("V", b))
            for b in (0, 1):
                wait(act, k("U", b), k("V", b))
                inc(act.activation(pT[b][:, 0:128], sS[b][:, 0:128], Exp, bias=nmo[b], scale=1.0), k("X", b))
        for b in (0, 1):
            wait(pe, *kdata)
            wait(pe, k("V", b), k("X", b), *old("USVXREF", b))
            for i in range(f, nb):
                inc(pe.matmul(sS[b][:, i * 128:(i + 1) * 128], qb[b], kv[:, i * BW:i * BW + 128], True, True),
                    k("S", b))
        for b in (0, 1):
            wait(dve, k("S", b), k("U", b), k("X", b))
            inc(dve.tensor_reduce(nm[b], sS[b][:, 0:n], AxisListType.X, AluOpType.max, negate=True), k("R", b))
        for b in (0, 1):
            wait(act, k("S", b), k("R", b))
            if own:
                inc(act.activation(T.wo[:, 4 * b:4 * b + 1], nmo[b], Exp, bias=nm[b], scale=-1.0), k("W", b))
            for x, (a, z, s) in enumerate(pieces):
                inc(act.activation(pT[b][:, a * 128:z * 128], sS[b][:, a * 128:z * 128], Exp, bias=nm[b], scale=1.0,
                                   accum_out=T.lw[:, 8 * b + NP + x:8 * b + NP + x + 1] if keep else None), k(s, b))
        if own:
            for b in (0, 1):
                wait(dve, k("W", b), "idn")
                inc(dve.tensor_scalar(T.dgo[:, b * 128:(b + 1) * 128], T.ident[:, :], T.wo[:, 4 * b:4 * b + 1], None,
                                      AluOpType.mult), k("D", b))
        for b in (0, 1):
            wait(pe, "idn", *old("TC", b))
            if own:
                wait(pe, k("D", b), k("X", b))
                inc(pe.matmul(tF[b][:, 0:128], pT[b][:, 0:128], T.dgo[:, b * 128:(b + 1) * 128], True, True),
                    k("G", b))
            for a, z, s in pieces:
                wait(pe, k(s, b))
                for i in range(a, z):
                    inc(pe.transpose(tP[b][:, i * 128:(i + 1) * 128], pT[b][:, i * 128:(i + 1) * 128],
                                     T.ident[:, :]), k("T", b))
        for b in (0, 1):
            if own:
                wait(dve, k("G", b))
                inc(dve.tensor_copy(pK[b][:, 0:128], tF[b][:, 0:128]), k("H", b))
            wait(dve, k("T", b))
            inc(dve.tensor_copy(pK[b][:, f * 128:n], tP[b][:, f * 128:n]), k("C", b))
        for b in (0, 1):
            wait(pe, *vdata)
            wait(pe, k("C", b), k("H", b), "ms", *old("OP", b))
            for i in range(nb):
                inc(pe.matmul(oP[b][:, 0:129], pK[b][:, i * 128:(i + 1) * 128], kv[:, i * BW + 128:i * BW + 257],
                              i == 0, i == nb - 1 and not keep), k("O", b))
        if keep:
            return
        for b in (0, 1):
            wait(act, k("O", b))
            inc(act.activation(dst[:, off + b * HB:off + b * HB + 129], oP[b][:, 0:129], Copy), k("P", b))

    if not is_root:
        group("A", 0, T.kvA, nA, T.msg, 0, T.sh, 0, ["arrA"], ["arrA"], None, [qsem, "ld"])
        s = hs.index(core)
        wait(g, "ms", "RA0", "RA1")
        send(root, T.stat[:, s * 8:(s + 1) * 8], T.sh[:, :], "arrM")
        wait(g, "PA0", "PA1")
        send(root, T.part[:, s * SW:(s + 1) * SW], T.msg[:, :], "aP%d" % s)
        wait(g, "sent")
        return

    nh = len(hs)
    sA, sL = nh, nh + 1
    group("A", 0, T.kvA, nA, T.part, sA * SW, T.stat, sA * 8, [qsem, "ld"], ["ld"], None, None)
    group("L", 1, T.kvL, len(plain), None, 0, T.stat, sL * 8, ["arrLk"], ["arrLv"], "A", None, keep=True)

    order = [sA] + list(range(nh))
    for b in (0, 1):
        wait(dve, "arrM", "RA%d" % b, "RL%d" % b)
        inc(dve.tensor_reduce(T.gM[:, 4 * b:4 * b + 1], T.stat[:, b:b + (NSLOT - 1) * 8 + 1:8], AxisListType.X,
                              AluOpType.min), "gm%d" % b)
    for b in (0, 1):
        wait(dve, "gm%d" % b)
        inc(dve.tensor_scalar(T.gB[:, 4 * b:4 * b + 1], T.gM[:, 4 * b:4 * b + 1], CLAMP,
                              T.stat[:, sL * 8 + b:sL * 8 + b + 1], AluOpType.add, AluOpType.min), "gb%d" % b)
        wait(act, "arrM", "RA%d" % b, "gb%d" % b)
        inc(act.activation(T.wj[:, 8 * b:8 * b + NP], T.stat[:, b:b + (NP - 1) * 8 + 1:8], Exp,
                           bias=T.gB[:, 4 * b:4 * b + 1], scale=-1.0), "gw%d" % b)
    wait(dve, "gw0", "idn")
    wait(act, "gw1", "idn")
    for j in order:
        c0, c1 = j * 128, (NP + j) * 128
        inc(dve.tensor_scalar(T.dg[:, c0:c0 + 128], T.ident[:, :], T.wj[:, j:j + 1], None, AluOpType.mult),
            "gd0%d" % j)
        inc(act.activation(T.dg[:, c1:c1 + 128], T.ident[:, :], Copy, scale=T.wj[:, 8 + j:8 + j + 1]), "gd1%d" % j)
    for x, j in enumerate(order):
        for b in (0, 1):
            wait(pe, "gd%d%d" % (b, j), "aP%d" % j if j < nh else "PA%d" % b)
            c = (b * NP + j) * 128
            inc(pe.matmul(oP[b][:, 0:129], T.dg[:, c:c + 128], T.part[:, j * SW + b * HB:j * SW + b * HB + 129],
                          False, x == NP - 1), "ga%d" % b)
    for b in (0, 1):
        wait(dve, "PA%d" % b, "gw%d" % b, *["aP%d" % j for j in range(nh)])
        inc(dve.tensor_tensor(T.lw[:, 8 * b:8 * b + NP], T.wj[:, 8 * b:8 * b + NP],
                              T.part[:, b * HB + 128:b * HB + 128 + (NP - 1) * SW + 1:SW], AluOpType.mult), "la%d" % b)
    for b in (0, 1):
        wait(dve, "la%d" % b, "EL%d" % b, "FL%d" % b)
        inc(dve.tensor_reduce(T.lt[:, b:b + 1], T.lw[:, 8 * b:8 * b + NP + 2], AxisListType.X, AluOpType.add),
            "lr%d" % b)
    wait(dve, "lr0", "lr1")
    inc(dve.reciprocal(T.rc[:, 0:2], T.lt[:, 0:2]), "gr")
    wait(dve, "OL0", "ga0", "gr")
    inc(dve.tensor_scalar(T.ys[:, 0:128], oP[0][:, 0:128], T.rc[:, 0:1], None, AluOpType.mult), "gy0")
    wait(act, "OL1", "ga1", "gr")
    inc(act.activation(T.ys[:, 128:256], oP[1][:, 0:128], Copy, scale=T.rc[:, 1:2]), "gy1")
    for b, q in ((0, g.sync), (1, act)):
        wait(q, "gy%d" % b)
        inc(q.dma_start(T.y[b * 128:(b + 1) * 128, :], T.ys[:, b * 128:(b + 1) * 128]), "st", 16)
    wait(g.sync, "st")
    wait(g, "sent")
